import numpy as np
import ml_dtypes


def mxq(x, axis, fmt="e4m3"):
    dtype, down = {"e4m3": (ml_dtypes.float8_e4m3fn, 7), "e5m2": (ml_dtypes.float8_e5m2, 14)}[fmt]
    v = np.moveaxis(np.asarray(x, np.float32).astype(ml_dtypes.bfloat16).astype(np.float64), axis, -1)
    blocks = v.reshape(v.shape[:-1] + (-1, 32))
    amax = np.abs(blocks).max(-1, keepdims=True)
    byte = np.maximum(np.where(amax > 0, np.frexp(amax)[1] - 1 + 127, 0) - down, 1)
    scale = np.exp2(byte - 127.0)
    codes = (blocks / scale).astype(np.float32).astype(dtype).astype(np.float64)
    return np.moveaxis((codes * scale).reshape(v.shape), -1, axis)


WIDE = False


def mx_kscale(k):
    if not WIDE:
        return np.ones(k)
    levels = np.array([10, -10, 5, -5, 0])
    if k % 512:
        return np.exp2(np.random.permutation(np.resize(levels, k // 32))).repeat(32)
    a = np.empty((k // 512, 16))
    for p in range(k // 512):
        a[p, :8] = np.random.permutation(np.resize(levels, 8))
        for g in range(8):
            far = levels[np.abs(levels - a[p, g]) >= 10]
            a[p, g + 8] = far[np.random.randint(len(far))]
    return np.exp2(a.ravel()).repeat(32)


BF16 = ml_dtypes.bfloat16


def bf(x):
    return np.asarray(x, np.float32).astype(BF16)


def f64(x):
    return np.asarray(x).astype(np.float64)


N, Z, D, H, V = 1536, 4, 512, 512, 1024


def logsumexp(t, axis, keepdims):
    m = t.max(axis=axis, keepdims=True)
    out = m + np.log(np.sum(np.exp(t - m), axis=axis, keepdims=True))
    return out if keepdims else np.squeeze(out, axis=axis)


def draw0():
    s, t = mx_kscale(D), mx_kscale(H)
    return {
        "x": bf(np.random.standard_normal((N, Z, D)) * s),
        "w1": bf(np.random.standard_normal((D, H)) / np.sqrt(D) / s[:, None]),
        "b1": bf(0.3 * np.random.standard_normal(H)),
        "g": bf((1.0 + 0.1 * np.random.standard_normal(H)) * t),
        "e": bf(2.0 * np.random.standard_normal((H, V)) / np.sqrt(H) / t[:, None]),
        "score": bf(np.random.standard_normal((N, Z))),
    }


def core(x, w1, b1, g, e, score):
    vocab = e.shape[1]
    a = np.tanh((mxq(f64(x), 2, "e4m3") @ mxq(f64(w1), 0, "e4m3")) + f64(b1)) * f64(g)
    logits = mxq(a, 2, "e4m3") @ mxq(f64(e), 0, "e4m3")
    lp = logits - logsumexp(logits, 2, True)
    sc = f64(score)
    prior = sc - logsumexp(sc, 1, True)
    return logsumexp(prior[:, :, None] + lp, 1, False) + np.log(vocab)


def e4m3fn_bytes(y):
    return np.clip(np.asarray(y, np.float64), -448.0, 448.0).astype(np.float32).astype(ml_dtypes.float8_e4m3fn).view(np.uint8)


def e4m3fn_values(b):
    return np.asarray(b, np.uint8).view(ml_dtypes.float8_e4m3fn).astype(np.float64)


def setup_inputs():
    d = draw0()
    x0 = np.asarray(d['x']).astype(np.float64)
    s = (np.max(np.abs(x0), axis=(0, 1), keepdims=True) / 448.0).astype(np.float32)
    out = {}
    for k, v in d.items():
        if k == 'x':
            out['x_bytes'] = e4m3fn_bytes(x0 / s.astype(np.float64))
            out['x_scale'] = s
        else:
            out[k] = v
    return out


def reference(x_bytes, x_scale, w1, b1, g, e, score):
    return core(e4m3fn_values(x_bytes) * x_scale.astype(np.float64), w1, b1, g, e, score)

@@ -1,0 +1,401 @@
+from contextlib import ExitStack
+
+import concourse.mybir as mybir
+from concourse.masks import make_identity
+
+N, Z, D, H, V = 1536, 4, 512, 512, 1024
+FLOPS = 2 * N * Z * (D * H + H * V)
+
+F32 = mybir.dt.float32
+BF16 = mybir.dt.bfloat16
+U32 = mybir.dt.uint32
+U8 = mybir.dt.uint8
+FP8 = mybir.dt.float8_e4m3fn
+FP8X4 = mybir.dt.float8_e4m3fn_x4
+ACT = mybir.ActivationFunctionType
+ALU = mybir.AluOpType
+AX = mybir.AxisListType
+
+P = 128
+PACK = 4
+BANK = 512
+TILES = N // P
+ROWS = Z * P
+HALVES = V // BANK
+BLOCKS = BANK // P
+RING = 4
+GAIN_ON_GPSIMD = False
+
+
+def tile_ragtokendocumentmarginal_t_kernel(tc, x_bytes, x_scale, w1, b1, g, e, score, out):
+    nc = tc.nc
+    x_tiles = x_bytes.rearrange("(p i) z d -> i p (z d)", i=TILES)
+    out_tiles = out.rearrange("(p i) v -> i p v", i=TILES)
+
+    with ExitStack() as ctx:
+        sb = ctx.enter_context(tc.tile_pool(name="sb", bufs=1))
+        ps = ctx.enter_context(tc.psum_pool(name="ps", bufs=1))
+        ctx.enter_context(tc.manual_schedule())
+
+        def ring(name, count, shape, dtype):
+            return [sb.tile(shape, dtype, name="%s%d" % (name, j), align_bytes=64) for j in range(count)]
+
+        def one(name, shape, dtype):
+            return sb.tile(shape, dtype, name=name, align_bytes=64)
+
+        vec_banks = [ps.tile([P, BANK], F32, name="vec_bank%d" % j) for j in range(RING)]
+        act_banks = [ps.tile([P, BANK], F32, name="act_bank%d" % j) for j in range(RING)]
+
+        x_code_bytes = ring("x_code_bytes", TILES, [P, Z * D], U8)
+        x_scale_rows = one("x_scale_rows", [P, D], F32)
+        w_raw = one("w_raw", [P, PACK, H], BF16)
+        w_grouped = one("w_grouped", [P, PACK * H], BF16)
+        w_codes = one("w_codes", [P, H], U32)
+        w_scales = one("w_scales", [P, H], U8)
+        e_raw = ring("e_raw", HALVES, [P, PACK, BANK], BF16)
+        e_grouped = ring("e_grouped", HALVES, [P, PACK * BANK], BF16)
+        e_codes = ring("e_codes", HALVES, [P, BANK], U32)
+        e_scales = ring("e_scales", HALVES, [P, BANK], U8)
+        bias_cols = one("bias_cols", [P, PACK], BF16)
+        gain_cols = one("gain_cols", [P, PACK], BF16)
+        identity = one("identity", [P, P], F32)
+
+        score_sb = one("score_sb", [P, TILES, Z], BF16)
+        score_max = one("score_max", [P, TILES], F32)
+        score_shifted = one("score_shifted", [P, TILES, Z], F32)
+        score_exp = one("score_exp", [P, TILES, Z], F32)
+        score_sum = one("score_sum", [P, TILES], F32)
+        score_norm = one("score_norm", [P, TILES], F32)
+
+        x_rows = ring("x_rows", 2, [P, Z * D], BF16)
+        x_grouped = ring("x_grouped", 2, [P, PACK * ROWS], BF16)
+        x_codes = ring("x_codes", 2, [P, ROWS], U32)
+        x_scales = ring("x_scales", 2, [P, ROWS], U8)
+        hidden = ring("hidden", 2, [P, PACK, ROWS], F32)
+        a_grouped = one("a_grouped", [P, PACK * ROWS], BF16)
+        a_codes = ring("a_codes", 4, [P, ROWS], U32)
+        a_scales = ring("a_scales", 4, [P, ROWS], U8)
+        neg_logits = ring("neg_logits", 2 * Z, [P, V], F32)
+        terms = ring("terms", 2 * Z, [P, V], F32)
+        neg_shift = ring("neg_shift", 4, [P, V], F32)
+        log_sum_t = ring("log_sum_t", 2, [P, V], F32)
+        result = ring("result", 2, [P, V], F32)
+        neg_half_max = ring("neg_half_max", TILES, [P, Z, HALVES], F32)
+        neg_max = ring("neg_max", TILES, [P, Z], F32)
+        offset = ring("offset", TILES, [P, Z], F32)
+        rel_offset = ring("rel_offset", TILES, [P, Z], F32)
+        row_sum = ring("row_sum", TILES, [P, Z], F32)
+        log_row_sum = ring("log_row_sum", TILES, [P, Z], F32)
+        neg_log_row_sum = ring("neg_log_row_sum", TILES, [P, Z], F32)
+
+        def exists(i):
+            return 0 <= i < TILES
+
+        def half(h):
+            return slice(h * BANK, (h + 1) * BANK)
+
+        def block(j):
+            return slice(j * P, (j + 1) * P)
+
+        nc.sync.dma_start(out=x_code_bytes[0][:], in_=x_tiles[0])
+        nc.sync.dma_start(out=x_scale_rows[:], in_=x_scale.rearrange("a b d -> (a b d)").partition_broadcast(P))
+        nc.sync.dma_start(out=w_raw[:], in_=w1.rearrange("(p j) c -> p j c", j=PACK))
+        nc.sync.dma_start(out=score_sb[:], in_=score.rearrange("(p i) z -> p i z", i=TILES))
+        nc.sync.dma_start(out=x_code_bytes[1][:], in_=x_tiles[1])
+        nc.sync.dma_start(out=bias_cols[:], in_=b1.rearrange("(p t) -> p t", t=PACK))
+        nc.sync.dma_start(out=gain_cols[:], in_=g.rearrange("(p t) -> p t", t=PACK))
+        for h in range(HALVES):
+            nc.sync.dma_start(out=e_raw[h][:], in_=e[:, half(h)].rearrange("(p j) n -> p j n", j=PACK))
+        for i in range(2, TILES):
+            nc.sync.dma_start(out=x_code_bytes[i][:], in_=x_tiles[i])
+        make_identity(nc, identity[:])
+
+        def group_w():
+            nc.vector.tensor_copy(
+                out=w_grouped[:].rearrange("p (t m j) -> p t m j", t=PACK, j=PACK),
+                in_=w_raw[:].rearrange("p j (m t) -> p t m j", t=PACK),
+            )
+
+        def group_e(copy, h):
+            copy(out=e_grouped[h][:].rearrange("p (n j) -> p n j", j=PACK), in_=e_raw[h][:].rearrange("p j n -> p n j"))
+
+        def quantize(codes, scales, grouped):
+            nc.vector.quantize_mx(out=codes[:].bitcast(FP8X4), scales=scales[:], in_=grouped[:])
+
+        def prior_shift():
+            nc.vector.tensor_reduce(out=score_max[:], in_=score_sb[:], axis=AX.X, op=ALU.max)
+            nc.vector.tensor_tensor(
+                out=score_shifted[:], in0=score_sb[:], in1=score_max[:].unsqueeze(2).to_broadcast([P, TILES, Z]), op=ALU.subtract
+            )
+            nc.scalar.activation(out=score_exp[:], in_=score_shifted[:], func=ACT.Exp)
+
+        def prior_sum():
+            nc.vector.tensor_reduce(out=score_sum[:], in_=score_exp[:], axis=AX.X, op=ALU.add)
+
+        def prior_finish():
+            nc.vector.tensor_scalar(out=score_norm[:], in0=score_sum[:], scalar1=1.0 / V, scalar2=None, op0=ALU.mult)
+
+        def scale_x(i):
+            nc.vector.tensor_tensor(
+                out=x_rows[i % 2][:].rearrange("p (z d) -> p z d", z=Z),
+                in0=x_code_bytes[i][:].bitcast(FP8).rearrange("p (z d) -> p z d", z=Z),
+                in1=x_scale_rows[:].unsqueeze(1).to_broadcast([P, Z, D]),
+                op=ALU.mult,
+            )
+
+        def turn_x(i):
+            words = x_rows[i % 2][:].bitcast(F32)
+            for z in range(Z):
+                for u in range(2):
+                    nc.tensor.transpose(
+                        act_banks[2 + z // 2][:, block(2 * (z % 2) + u)],
+                        words[:, z * D // 2 + u : (z + 1) * D // 2 : 2],
+                        identity[:],
+                    )
+
+        def group_x(i):
+            words = x_grouped[i % 2][:].bitcast(F32)
+            for b in range(2):
+                nc.scalar.copy(
+                    out=words[:, half(b)].rearrange("p (z r u) -> p z r u", z=2, u=2),
+                    in_=act_banks[2 + b][:].rearrange("p (z u r) -> p z r u", z=2, u=2),
+                )
+
+        def first_product(i, t):
+            nc.tensor.matmul_mx(
+                out=act_banks[t][:],
+                lhsT=w_codes[:, block(t)].bitcast(FP8X4),
+                lhsT_scale=w_scales[:, block(t)],
+                rhs=x_codes[i % 2][:].bitcast(FP8X4),
+                rhs_scale=x_scales[i % 2][:],
+                start=True,
+                stop=True,
+            )
+
+        def activate(i):
+            for t in range(PACK):
+                nc.scalar.activation(out=hidden[i % 2][:, t, :], in_=act_banks[t][:], func=ACT.Tanh, bias=bias_cols[:, t : t + 1])
+
+        def apply_gain(engine, i):
+            engine.tensor_tensor(
+                out=a_grouped[:].rearrange("p (r t) -> p r t", t=PACK),
+                in0=hidden[i % 2][:].rearrange("p t r -> p r t"),
+                in1=gain_cols[:].unsqueeze(1).to_broadcast([P, ROWS, PACK]),
+                op=ALU.mult,
+            )
+
+        def logits(bank, i, z, h):
+            nc.tensor.matmul_mx(
+                out=bank[:],
+                lhsT=a_codes[i % 4][:, block(z)].bitcast(FP8X4),
+                lhsT_scale=a_scales[i % 4][:, block(z)],
+                rhs=e_codes[h][:].bitcast(FP8X4),
+                rhs_scale=e_scales[h][:],
+                start=True,
+                stop=True,
+            )
+
+        def take_max(bank, i, z, h):
+            nc.vector.tensor_scalar(
+                out=neg_logits[(i % 2) * Z + z][:, half(h)],
+                in0=bank[:],
+                scalar1=-1.0,
+                scalar2=None,
+                op0=ALU.mult,
+                op1=ALU.min,
+                accum_out=neg_half_max[i][:, z, h : h + 1],
+            )
+
+        def shift_logits(bank, i, z, h):
+            nc.vector.scalar_tensor_tensor(
+                out=terms[(i % 2) * Z + z][:, half(h)],
+                in0=bank[:],
+                scalar=rel_offset[i][:, z : z + 1],
+                in1=neg_shift[i % 4][:, half(h)],
+                op0=ALU.add,
+                op1=ALU.add,
+            )
+
+        def turn_back(bank, i, z, h):
+            for j in range(BLOCKS):
+                nc.tensor.transpose(bank[:, block(j)], log_sum_t[i % 2][:, block(h * BLOCKS + j)], identity[:])
+
+        def finish(bank, i, z, h):
+            nc.vector.scalar_tensor_tensor(
+                out=result[i % 2][:, half(h)],
+                in0=bank[:],
+                scalar=offset[i][:, 0:1],
+                in1=neg_shift[i % 4][:, half(h)],
+                op0=ALU.add,
+                op1=ALU.subtract,
+            )
+            nc.sync.dma_start(out=out_tiles[i][:, half(h)], in_=result[i % 2][:, half(h)])
+
+        last = TILES - 1
+
+        def summed_in(s):
+            return [last - 1, last] if s == last else [i for i in [s - 1] if 0 <= i < last - 1]
+
+        def mixed_in(s):
+            return summed_in(s - 1)
+
+        def finished_in(s):
+            return summed_in(s - 2)
+
+        def sum_bank(i, h):
+            return act_banks[(HALVES if i == last else 0) + h]
+
+        def step_jobs(s):
+            jobs = [(logits, shift_logits, i, z, h) for i in mixed_in(s) for z in range(Z) for h in range(HALVES)]
+            if exists(s):
+                jobs.extend((logits, take_max, s, z, h) for z in range(Z) for h in range(HALVES))
+            jobs.extend((turn_back, finish, i, 0, h) for i in finished_in(s) for h in range(HALVES))
+            return jobs
+
+        steps = range(-4, TILES + 2)
+        all_jobs = [(s, job) for s in steps for job in step_jobs(s)]
+        count = {"filled": 0, "emptied": 0}
+
+        def fill_ahead(s):
+            while count["filled"] < min(count["emptied"] + RING, len(all_jobs)):
+                job_step, (fill, empty, i, z, h) = all_jobs[count["filled"]]
+                if job_step > s and empty != shift_logits:
+                    break
+                fill(vec_banks[count["filled"] % RING], i, z, h)
+                count["filled"] = count["filled"] + 1
+
+        def empty_jobs(s, number):
+            for k in range(number):
+                fill_ahead(s)
+                job_step, (fill, empty, i, z, h) = all_jobs[count["emptied"]]
+                empty(vec_banks[count["emptied"] % RING], i, z, h)
+                count["emptied"] = count["emptied"] + 1
+            fill_ahead(s)
+
+        def row_max(i):
+            nc.vector.tensor_reduce(out=neg_max[i][:], in_=neg_half_max[i][:], axis=AX.X, op=ALU.min)
+
+        def row_offset(i):
+            nc.vector.tensor_tensor(out=offset[i][:], in0=neg_max[i][:], in1=score_shifted[:, i, :], op=ALU.add)
+
+        def row_rel_offset(i):
+            nc.vector.tensor_scalar(
+                out=rel_offset[i][:], in0=offset[i][:], scalar1=offset[i][:, 0:1], scalar2=None, op0=ALU.subtract
+            )
+
+        def fold_shift(i, z):
+            so_far = neg_logits[(i % 2) * Z] if z == 1 else neg_shift[i % 4]
+            nc.vector.scalar_tensor_tensor(
+                out=neg_shift[i % 4][:],
+                in0=neg_logits[(i % 2) * Z + z][:],
+                scalar=rel_offset[i][:, z : z + 1],
+                in1=so_far[:],
+                op0=ALU.subtract,
+                op1=ALU.min,
+            )
+
+        def sum_rows(i):
+            for z in range(Z):
+                tile = neg_logits[(i % 2) * Z + z]
+                nc.scalar.activation(
+                    out=tile[:], in_=tile[:], func=ACT.Exp, scale=-1.0, bias=neg_max[i][:, z : z + 1], accum_out=row_sum[i][:, z : z + 1]
+                )
+
+        def exp_term(i, z):
+            tile = terms[(i % 2) * Z + z]
+            nc.scalar.activation(out=tile[:], in_=tile[:], func=ACT.Exp, bias=neg_log_row_sum[i][:, z : z + 1])
+
+        def add_term(i, z):
+            for h in range(HALVES):
+                for j in range(BLOCKS):
+                    nc.tensor.matmul(
+                        out=sum_bank(i, h)[:, block(j)],
+                        lhsT=terms[(i % 2) * Z + z][:, block(h * BLOCKS + j)],
+                        rhs=identity[:],
+                        is_transpose=True,
+                        start=(z == 0 and j == 0),
+                        stop=(z == Z - 1 and j == BLOCKS - 1),
+                    )
+
+        def logarithms(s):
+            for i in summed_in(s):
+                nc.scalar.activation(out=log_row_sum[i][:], in_=row_sum[i][:], func=ACT.Ln, scale=score_norm[:, i : i + 1])
+            for i in mixed_in(s):
+                for h in range(HALVES):
+                    nc.scalar.activation(out=log_sum_t[i % 2][:, half(h)], in_=sum_bank(i, h)[:], func=ACT.Ln)
+            for i in summed_in(s):
+                nc.scalar.activation(out=neg_log_row_sum[i][:], in_=log_row_sum[i][:], func=ACT.Copy, scale=-1.0)
+
+        for s in steps:
+            if exists(s):
+                quantize(a_codes[s % 4], a_scales[s % 4], a_grouped)
+            if exists(s + 1):
+                activate(s + 1)
+                if GAIN_ON_GPSIMD and s >= 0:
+                    apply_gain(nc.gpsimd, s + 1)
+            for i in mixed_in(s):
+                for z in range(Z):
+                    empty_jobs(s, HALVES)
+                    exp_term(i, z)
+            if exists(s):
+                empty_jobs(s, 2)
+                for z in range(2):
+                    empty_jobs(s, 2)
+                    for i in mixed_in(s):
+                        add_term(i, z)
+                empty_jobs(s, 2)
+                row_max(s)
+            if finished_in(s):
+                empty_jobs(s, 1)
+            if exists(s):
+                row_offset(s)
+            if finished_in(s):
+                empty_jobs(s, HALVES * len(finished_in(s)) - 1)
+            if exists(s):
+                for i in mixed_in(s):
+                    add_term(i, 2)
+                    add_term(i, 3)
+                row_rel_offset(s)
+            if exists(s + 3):
+                turn_x(s + 3)
+            if s == TILES:
+                for i in mixed_in(s):
+                    for z in range(Z):
+                        add_term(i, z)
+            if exists(s + 2):
+                quantize(x_codes[s % 2], x_scales[s % 2], x_grouped[s % 2])
+            if exists(s):
+                fold_shift(s, 1)
+            if exists(s + 1) and not (GAIN_ON_GPSIMD and s >= 0):
+                apply_gain(nc.vector, s + 1)
+            if exists(s):
+                fold_shift(s, 2)
+            if exists(s + 4):
+                scale_x(s + 4)
+            if exists(s):
+                fold_shift(s, 3)
+            for i in summed_in(s):
+                sum_rows(i)
+            if s == -4:
+                group_w()
+                prior_shift()
+                quantize(w_codes, w_scales, w_grouped)
+            if s == -3:
+                prior_sum()
+            if s == -2:
+                group_e(nc.vector.tensor_copy, 0)
+                prior_finish()
+                quantize(e_codes[0], e_scales[0], e_grouped[0])
+            if s == -1:
+                quantize(e_codes[1], e_scales[1], e_grouped[1])
+            logarithms(s)
+            if exists(s + 2):
+                first_product(s + 2, 0)
+                first_product(s + 2, 1)
+            if exists(s + 3):
+                group_x(s + 3)
+            if exists(s + 2):
+                first_product(s + 2, 2)
+                first_product(s + 2, 3)
+            if s == -2:
+                group_e(nc.scalar.copy, 1)

@@ -24,7 +24,7 @@ ROWS = Z * P
 HALVES = V // BANK
 BLOCKS = BANK // P
 RING = 4
-GAIN_ON_GPSIMD = False
+GAIN_ON_GPSIMD = True
 
 
 def tile_ragtokendocumentmarginal_t_kernel(tc, x_bytes, x_scale, w1, b1, g, e, score, out):

@@ -24,7 +24,8 @@ ROWS = Z * P
 HALVES = V // BANK
 BLOCKS = BANK // P
 RING = 4
-GAIN_ON_GPSIMD = True
+TERM_ORDER = (1, 2, 0, 3)
+LOG_STEPS = [1, 3, 5, 7, 9, 10, 12]
 
 
 def tile_ragtokendocumentmarginal_t_kernel(tc, x_bytes, x_scale, w1, b1, g, e, score, out):
@@ -47,6 +48,7 @@ def tile_ragtokendocumentmarginal_t_kernel(tc, x_bytes, x_scale, w1, b1, g, e, s
         act_banks = [ps.tile([P, BANK], F32, name="act_bank%d" % j) for j in range(RING)]
 
         x_code_bytes = ring("x_code_bytes", TILES, [P, Z * D], U8)
+        x_scale_cols = one("x_scale_cols", [P, PACK], F32)
         x_scale_rows = one("x_scale_rows", [P, D], F32)
         w_raw = one("w_raw", [P, PACK, H], BF16)
         w_grouped = one("w_grouped", [P, PACK * H], BF16)
@@ -75,7 +77,8 @@ def tile_ragtokendocumentmarginal_t_kernel(tc, x_bytes, x_scale, w1, b1, g, e, s
         a_grouped = one("a_grouped", [P, PACK * ROWS], BF16)
         a_codes = ring("a_codes", 4, [P, ROWS], U32)
         a_scales = ring("a_scales", 4, [P, ROWS], U8)
-        neg_logits = ring("neg_logits", 2 * Z, [P, V], F32)
+        neg_logits = ring("neg_logits", Z + 1, [P, V], F32)
+        exp_unused = ring("exp_unused", 2, [P, V], BF16)
         terms = ring("terms", 2 * Z, [P, V], F32)
         neg_shift = ring("neg_shift", 4, [P, V], F32)
         log_sum_t = ring("log_sum_t", 2, [P, V], F32)
@@ -88,8 +91,14 @@ def tile_ragtokendocumentmarginal_t_kernel(tc, x_bytes, x_scale, w1, b1, g, e, s
         log_row_sum = ring("log_row_sum", TILES, [P, Z], F32)
         neg_log_row_sum = ring("neg_log_row_sum", TILES, [P, Z], F32)
 
+        last_norm = one("last_norm", [P, Z], F32)
+        last_weight = one("last_weight", [P, Z], F32)
+
         def exists(i):
             return 0 <= i < TILES
+
+        def neg_logits_of(i, z):
+            return neg_logits[z if z > 0 else Z * (i % 2)]
 
         def half(h):
             return slice(h * BANK, (h + 1) * BANK)
@@ -97,10 +106,10 @@ def tile_ragtokendocumentmarginal_t_kernel(tc, x_bytes, x_scale, w1, b1, g, e, s
         def block(j):
             return slice(j * P, (j + 1) * P)
 
-        nc.sync.dma_start(out=x_code_bytes[0][:], in_=x_tiles[0])
-        nc.sync.dma_start(out=x_scale_rows[:], in_=x_scale.rearrange("a b d -> (a b d)").partition_broadcast(P))
-        nc.sync.dma_start(out=w_raw[:], in_=w1.rearrange("(p j) c -> p j c", j=PACK))
+        nc.sync.dma_start(out=x_scale_cols[:], in_=x_scale.rearrange("a b (p j) -> p (a b j)", j=PACK))
         nc.sync.dma_start(out=score_sb[:], in_=score.rearrange("(p i) z -> p i z", i=TILES))
+        nc.sync.dma_start(out=x_code_bytes[0][:], in_=x_tiles[0])
+        nc.sync.dma_start(out=w_raw[:], in_=w1.rearrange("(p j) c -> p j c", j=PACK))
         nc.sync.dma_start(out=x_code_bytes[1][:], in_=x_tiles[1])
         nc.sync.dma_start(out=bias_cols[:], in_=b1.rearrange("(p t) -> p t", t=PACK))
         nc.sync.dma_start(out=gain_cols[:], in_=g.rearrange("(p t) -> p t", t=PACK))
@@ -109,6 +118,13 @@ def tile_ragtokendocumentmarginal_t_kernel(tc, x_bytes, x_scale, w1, b1, g, e, s
         for i in range(2, TILES):
             nc.sync.dma_start(out=x_code_bytes[i][:], in_=x_tiles[i])
         make_identity(nc, identity[:])
+
+        def spread_x_scale():
+            for j in range(PACK):
+                nc.tensor.transpose(vec_banks[0][:, block(j)], x_scale_cols[:, j : j + 1].to_broadcast([P, P]), identity[:])
+            nc.scalar.copy(
+                out=x_scale_rows[:].rearrange("p (n j) -> p n j", j=PACK), in_=vec_banks[0][:].rearrange("p (j n) -> p n j", j=PACK)
+            )
 
         def group_w():
             nc.vector.tensor_copy(
@@ -143,12 +159,15 @@ def tile_ragtokendocumentmarginal_t_kernel(tc, x_bytes, x_scale, w1, b1, g, e, s
                 op=ALU.mult,
             )
 
-        def turn_x(i):
+        def front_bank(i, b):
+            return act_banks[b if i == 1 else 2 + b]
+
+        def turn_x(i, b):
             words = x_rows[i % 2][:].bitcast(F32)
-            for z in range(Z):
+            for z in range(2 * b, 2 * b + 2):
                 for u in range(2):
                     nc.tensor.transpose(
-                        act_banks[2 + z // 2][:, block(2 * (z % 2) + u)],
+                        front_bank(i, b)[:, block(2 * (z % 2) + u)],
                         words[:, z * D // 2 + u : (z + 1) * D // 2 : 2],
                         identity[:],
                     )
@@ -158,12 +177,12 @@ def tile_ragtokendocumentmarginal_t_kernel(tc, x_bytes, x_scale, w1, b1, g, e, s
             for b in range(2):
                 nc.scalar.copy(
                     out=words[:, half(b)].rearrange("p (z r u) -> p z r u", z=2, u=2),
-                    in_=act_banks[2 + b][:].rearrange("p (z u r) -> p z r u", z=2, u=2),
+                    in_=front_bank(i, b)[:].rearrange("p (z u r) -> p z r u", z=2, u=2),
                 )
 
         def first_product(i, t):
             nc.tensor.matmul_mx(
-                out=act_banks[t][:],
+                out=front_bank(i, t % 2)[:],
                 lhsT=w_codes[:, block(t)].bitcast(FP8X4),
                 lhsT_scale=w_scales[:, block(t)],
                 rhs=x_codes[i % 2][:].bitcast(FP8X4),
@@ -172,9 +191,8 @@ def tile_ragtokendocumentmarginal_t_kernel(tc, x_bytes, x_scale, w1, b1, g, e, s
                 stop=True,
             )
 
-        def activate(i):
-            for t in range(PACK):
-                nc.scalar.activation(out=hidden[i % 2][:, t, :], in_=act_banks[t][:], func=ACT.Tanh, bias=bias_cols[:, t : t + 1])
+        def activate(i, t):
+            nc.scalar.activation(out=hidden[i % 2][:, t, :], in_=front_bank(i, t % 2)[:], func=ACT.Tanh, bias=bias_cols[:, t : t + 1])
 
         def apply_gain(engine, i):
             engine.tensor_tensor(
@@ -197,7 +215,7 @@ def tile_ragtokendocumentmarginal_t_kernel(tc, x_bytes, x_scale, w1, b1, g, e, s
 
         def take_max(bank, i, z, h):
             nc.vector.tensor_scalar(
-                out=neg_logits[(i % 2) * Z + z][:, half(h)],
+                out=neg_logits_of(i, z)[:, half(h)],
                 in0=bank[:],
                 scalar1=-1.0,
                 scalar2=None,
@@ -232,34 +250,43 @@ def tile_ragtokendocumentmarginal_t_kernel(tc, x_bytes, x_scale, w1, b1, g, e, s
             nc.sync.dma_start(out=out_tiles[i][:, half(h)], in_=result[i % 2][:, half(h)])
 
         last = TILES - 1
+        steps = range(TILES + 2)
 
-        def summed_in(s):
-            return [last - 1, last] if s == last else [i for i in [s - 1] if 0 <= i < last - 1]
+        def next_log_step(s):
+            return min(x for x in LOG_STEPS if x >= s)
+
+        def spread(ready):
+            when = []
+            for i in range(TILES):
+                when.append(max(ready[i], min(when[-1] + 1, TILES - 2)) if when else ready[i])
+            return when
+
+        mix_step = spread([next_log_step(i) + 1 for i in range(last)] + [TILES])
+        finish_step = spread([next_log_step(mix_step[i]) + 1 for i in range(TILES)])
 
         def mixed_in(s):
-            return summed_in(s - 1)
+            return [i for i in range(TILES) if mix_step[i] == s]
 
         def finished_in(s):
-            return summed_in(s - 2)
+            return [i for i in range(TILES) if finish_step[i] == s]
 
         def sum_bank(i, h):
-            return act_banks[(HALVES if i == last else 0) + h]
+            return act_banks[HALVES * (1 if i == last else mixed_in(mix_step[i]).index(i)) + h]
 
         def step_jobs(s):
-            jobs = [(logits, shift_logits, i, z, h) for i in mixed_in(s) for z in range(Z) for h in range(HALVES)]
+            jobs = [(logits, shift_logits, i, z, h) for i in mixed_in(s) for z in range(1, Z) for h in range(HALVES)]
             if exists(s):
                 jobs.extend((logits, take_max, s, z, h) for z in range(Z) for h in range(HALVES))
             jobs.extend((turn_back, finish, i, 0, h) for i in finished_in(s) for h in range(HALVES))
             return jobs
 
-        steps = range(-4, TILES + 2)
         all_jobs = [(s, job) for s in steps for job in step_jobs(s)]
-        count = {"filled": 0, "emptied": 0}
+        count = {"filled": 0, "emptied": 0, "quantized": -1}
 
         def fill_ahead(s):
             while count["filled"] < min(count["emptied"] + RING, len(all_jobs)):
                 job_step, (fill, empty, i, z, h) = all_jobs[count["filled"]]
-                if job_step > s and empty != shift_logits:
+                if job_step > s and (empty == finish or i > count["quantized"]):
                     break
                 fill(vec_banks[count["filled"] % RING], i, z, h)
                 count["filled"] = count["filled"] + 1
@@ -283,27 +310,46 @@ def tile_ragtokendocumentmarginal_t_kernel(tc, x_bytes, x_scale, w1, b1, g, e, s
                 out=rel_offset[i][:], in0=offset[i][:], scalar1=offset[i][:, 0:1], scalar2=None, op0=ALU.subtract
             )
 
-        def fold_shift(i, z):
-            so_far = neg_logits[(i % 2) * Z] if z == 1 else neg_shift[i % 4]
+        def fold_shift(i, z, h):
+            so_far = neg_logits_of(i, 0) if z == 1 else neg_shift[i % 4]
             nc.vector.scalar_tensor_tensor(
-                out=neg_shift[i % 4][:],
-                in0=neg_logits[(i % 2) * Z + z][:],
+                out=neg_shift[i % 4][:, half(h)],
+                in0=neg_logits_of(i, z)[:, half(h)],
                 scalar=rel_offset[i][:, z : z + 1],
-                in1=so_far[:],
+                in1=so_far[:, half(h)],
                 op0=ALU.subtract,
                 op1=ALU.min,
             )
 
-        def sum_rows(i):
-            for z in range(Z):
-                tile = neg_logits[(i % 2) * Z + z]
-                nc.scalar.activation(
-                    out=tile[:], in_=tile[:], func=ACT.Exp, scale=-1.0, bias=neg_max[i][:, z : z + 1], accum_out=row_sum[i][:, z : z + 1]
-                )
+        def sum_row(i, z):
+            nc.scalar.activation(
+                out=exp_unused[z % 2][:],
+                in_=neg_logits_of(i, z)[:],
+                func=ACT.Exp,
+                scale=-1.0,
+                bias=neg_max[i][:, z : z + 1],
+                accum_out=row_sum[i][:, z : z + 1],
+            )
+
+        def shift_first_document(i):
+            nc.gpsimd.tensor_tensor(out=terms[(i % 2) * Z][:], in0=neg_shift[i % 4][:], in1=neg_logits_of(i, 0)[:], op=ALU.subtract)
 
         def exp_term(i, z):
             tile = terms[(i % 2) * Z + z]
-            nc.scalar.activation(out=tile[:], in_=tile[:], func=ACT.Exp, bias=neg_log_row_sum[i][:, z : z + 1])
+            if i < last:
+                nc.scalar.activation(out=tile[:], in_=tile[:], func=ACT.Exp, bias=neg_log_row_sum[i][:, z : z + 1])
+            else:
+                nc.scalar.activation(out=tile[:], in_=tile[:], func=ACT.Exp)
+
+        def last_weights():
+            nc.vector.tensor_scalar(
+                out=last_norm[:], in0=row_sum[last][:], scalar1=score_norm[:, last : last + 1], scalar2=None, op0=ALU.mult
+            )
+            nc.vector.reciprocal(out=last_weight[:], in_=last_norm[:])
+
+        def weigh_last_term(z):
+            tile = terms[(last % 2) * Z + z]
+            nc.vector.tensor_scalar(out=tile[:], in0=tile[:], scalar1=last_weight[:, z : z + 1], scalar2=None, op0=ALU.mult)
 
         def add_term(i, z):
             for h in range(HALVES):
@@ -313,89 +359,141 @@ def tile_ragtokendocumentmarginal_t_kernel(tc, x_bytes, x_scale, w1, b1, g, e, s
                         lhsT=terms[(i % 2) * Z + z][:, block(h * BLOCKS + j)],
                         rhs=identity[:],
                         is_transpose=True,
-                        start=(z == 0 and j == 0),
-                        stop=(z == Z - 1 and j == BLOCKS - 1),
+                        start=(z == TERM_ORDER[0] and j == 0),
+                        stop=(z == TERM_ORDER[-1] and j == BLOCKS - 1),
                     )
 
         def logarithms(s):
-            for i in summed_in(s):
+            rows = [i for i in range(last) if next_log_step(i) == s]
+            for i in rows:
                 nc.scalar.activation(out=log_row_sum[i][:], in_=row_sum[i][:], func=ACT.Ln, scale=score_norm[:, i : i + 1])
-            for i in mixed_in(s):
+            for i in range(TILES):
+                if mix_step[i] < min(s, last) and s == next_log_step(mix_step[i]):
+                    nc.scalar.activation(out=log_sum_t[i % 2][:], in_=log_sum_t[i % 2][:], func=ACT.Ln)
+            for i in mixed_in(s) if s < TILES else mixed_in(last) + mixed_in(s):
                 for h in range(HALVES):
                     nc.scalar.activation(out=log_sum_t[i % 2][:, half(h)], in_=sum_bank(i, h)[:], func=ACT.Ln)
-            for i in summed_in(s):
+            for i in rows:
                 nc.scalar.activation(out=neg_log_row_sum[i][:], in_=log_row_sum[i][:], func=ACT.Copy, scale=-1.0)
 
-        for s in steps:
-            if exists(s):
-                quantize(a_codes[s % 4], a_scales[s % 4], a_grouped)
-            if exists(s + 1):
-                activate(s + 1)
-                if GAIN_ON_GPSIMD and s >= 0:
-                    apply_gain(nc.gpsimd, s + 1)
+        def park_sums(s):
             for i in mixed_in(s):
-                for z in range(Z):
+                for h in range(HALVES):
+                    nc.scalar.copy(out=log_sum_t[i % 2][:, half(h)], in_=sum_bank(i, h)[:])
+
+        def quantize_x(i):
+            quantize(x_codes[i % 2], x_scales[i % 2], x_grouped[i % 2])
+
+        def quantize_a(i):
+            quantize(a_codes[i % 4], a_scales[i % 4], a_grouped)
+            count["quantized"] = i
+
+        def hidden_first_half(i):
+            for t in range(2):
+                first_product(i, t)
+            for t in range(2):
+                activate(i, t)
+                first_product(i, t + 2)
+
+        def hidden_second_half(i):
+            for t in range(2, PACK):
+                activate(i, t)
+
+        spread_x_scale()
+        prior_shift()
+        scale_x(0)
+        for b in range(2):
+            turn_x(0, b)
+        group_x(0)
+        prior_sum()
+        group_w()
+        prior_finish()
+        quantize(w_codes, w_scales, w_grouped)
+        scale_x(1)
+        for b in range(2):
+            turn_x(1, b)
+        quantize_x(0)
+        group_x(1)
+        hidden_first_half(0)
+        hidden_second_half(0)
+        group_e(nc.vector.tensor_copy, 0)
+        quantize_x(1)
+        group_e(nc.vector.tensor_copy, 1)
+        hidden_first_half(1)
+        hidden_second_half(1)
+        apply_gain(nc.vector, 0)
+        for h in range(HALVES):
+            quantize(e_codes[h], e_scales[h], e_grouped[h])
+        quantize_a(0)
+
+        for s in steps:
+            if exists(s - 1):
+                shift_first_document(s - 1)
+            if exists(s + 1):
+                apply_gain(nc.gpsimd, s + 1)
+            for b in range(2):
+                if mixed_in(s):
                     empty_jobs(s, HALVES)
+                if s > 0 and exists(s + 2):
+                    turn_x(s + 2, b)
+            if s > 0 and exists(s + 2):
+                group_x(s + 2)
+            if mixed_in(s):
+                empty_jobs(s, (Z - 1) * HALVES * len(mixed_in(s)) - 2 * HALVES)
+            for i in mixed_in(s):
+                for z in TERM_ORDER:
                     exp_term(i, z)
             if exists(s):
-                empty_jobs(s, 2)
-                for z in range(2):
+                empty_jobs(s, 4)
+                for z in TERM_ORDER[:2]:
                     empty_jobs(s, 2)
-                    for i in mixed_in(s):
+                    for i in mixed_in(s)[:1]:
                         add_term(i, z)
-                empty_jobs(s, 2)
-                row_max(s)
             if finished_in(s):
                 empty_jobs(s, 1)
             if exists(s):
-                row_offset(s)
+                row_max(s)
             if finished_in(s):
-                empty_jobs(s, HALVES * len(finished_in(s)) - 1)
+                empty_jobs(s, HALVES - 1)
+            if s == TILES:
+                last_weights()
+            for i in mixed_in(s):
+                for z in TERM_ORDER[2 if exists(s) and i == mixed_in(s)[0] else 0 :]:
+                    if i == last:
+                        weigh_last_term(z)
+                    add_term(i, z)
             if exists(s):
-                for i in mixed_in(s):
-                    add_term(i, 2)
-                    add_term(i, 3)
+                row_offset(s)
+                for z in range(Z - 1):
+                    sum_row(s, z)
+            if s == 0:
+                scale_x(2)
+                for b in range(2):
+                    turn_x(2, b)
+                group_x(2)
+            if s > 0 and exists(s + 2):
+                quantize_x(s + 2)
+                hidden_first_half(s + 2)
+            if exists(s):
                 row_rel_offset(s)
             if exists(s + 3):
-                turn_x(s + 3)
-            if s == TILES:
-                for i in mixed_in(s):
-                    for z in range(Z):
-                        add_term(i, z)
-            if exists(s + 2):
-                quantize(x_codes[s % 2], x_scales[s % 2], x_grouped[s % 2])
+                scale_x(s + 3)
+            if s == 0:
+                quantize_x(s + 2)
+                hidden_first_half(s + 2)
             if exists(s):
-                fold_shift(s, 1)
-            if exists(s + 1) and not (GAIN_ON_GPSIMD and s >= 0):
-                apply_gain(nc.vector, s + 1)
-            if exists(s):
-                fold_shift(s, 2)
-            if exists(s + 4):
-                scale_x(s + 4)
-            if exists(s):
-                fold_shift(s, 3)
-            for i in summed_in(s):
-                sum_rows(i)
-            if s == -4:
-                group_w()
-                prior_shift()
-                quantize(w_codes, w_scales, w_grouped)
-            if s == -3:
-                prior_sum()
-            if s == -2:
-                group_e(nc.vector.tensor_copy, 0)
-                prior_finish()
-                quantize(e_codes[0], e_scales[0], e_grouped[0])
-            if s == -1:
-                quantize(e_codes[1], e_scales[1], e_grouped[1])
-            logarithms(s)
+                sum_row(s, Z - 1)
             if exists(s + 2):
-                first_product(s + 2, 0)
-                first_product(s + 2, 1)
-            if exists(s + 3):
-                group_x(s + 3)
-            if exists(s + 2):
-                first_product(s + 2, 2)
-                first_product(s + 2, 3)
-            if s == -2:
-                group_e(nc.scalar.copy, 1)
+                hidden_second_half(s + 2)
+            if exists(s):
+                for z in range(1, Z):
+                    for h in range(HALVES):
+                        fold_shift(s, z, h)
+            if exists(s + 1):
+                quantize_a(s + 1)
+            empty_jobs(s, HALVES * len(finished_in(s)[1:]))
+            fill_ahead(s)
+            if s in LOG_STEPS:
+                logarithms(s)
+            elif s < last:
+                park_sums(s)

@@ -20,12 +20,19 @@ P = 128
 PACK = 4
 BANK = 512
 TILES = N // P
+LAST = TILES - 1
 ROWS = Z * P
 HALVES = V // BANK
 BLOCKS = BANK // P
+PAIRS = Z // 2
 RING = 4
+LIVE = 4
 TERM_ORDER = (1, 2, 0, 3)
-LOG_STEPS = [1, 3, 5, 7, 9, 10, 12]
+EARLY_TERMS = TERM_ORDER[:2]
+LATE_TERMS = TERM_ORDER[2:]
+MIX_LAG = 2
+FINISH_LAG = 4
+CATCH_UP = TILES - 2
 
 
 def tile_ragtokendocumentmarginal_t_kernel(tc, x_bytes, x_scale, w1, b1, g, e, score, out):
@@ -45,7 +52,7 @@ def tile_ragtokendocumentmarginal_t_kernel(tc, x_bytes, x_scale, w1, b1, g, e, s
             return sb.tile(shape, dtype, name=name, align_bytes=64)
 
         vec_banks = [ps.tile([P, BANK], F32, name="vec_bank%d" % j) for j in range(RING)]
-        act_banks = [ps.tile([P, BANK], F32, name="act_bank%d" % j) for j in range(RING)]
+        act_banks = [ps.tile([P, BANK], F32, name="act_bank%d" % j) for j in range(2 * HALVES)]
 
         x_code_bytes = ring("x_code_bytes", TILES, [P, Z * D], U8)
         x_scale_cols = one("x_scale_cols", [P, PACK], F32)
@@ -75,30 +82,29 @@ def tile_ragtokendocumentmarginal_t_kernel(tc, x_bytes, x_scale, w1, b1, g, e, s
         x_scales = ring("x_scales", 2, [P, ROWS], U8)
         hidden = ring("hidden", 2, [P, PACK, ROWS], F32)
         a_grouped = one("a_grouped", [P, PACK * ROWS], BF16)
-        a_codes = ring("a_codes", 4, [P, ROWS], U32)
-        a_scales = ring("a_scales", 4, [P, ROWS], U8)
+        a_codes = ring("a_codes", LIVE, [P, ROWS], U32)
+        a_scales = ring("a_scales", LIVE, [P, ROWS], U8)
         neg_logits = ring("neg_logits", Z + 1, [P, V], F32)
         exp_unused = ring("exp_unused", 2, [P, V], BF16)
         terms = ring("terms", 2 * Z, [P, V], F32)
-        neg_shift = ring("neg_shift", 4, [P, V], F32)
-        log_sum_t = ring("log_sum_t", 2, [P, V], F32)
+        neg_shift = ring("neg_shift", LIVE, [P, V], F32)
+        log_sum = ring("log_sum", 2, [P, V], F32)
         result = ring("result", 2, [P, V], F32)
         neg_half_max = ring("neg_half_max", TILES, [P, Z, HALVES], F32)
         neg_max = ring("neg_max", TILES, [P, Z], F32)
         offset = ring("offset", TILES, [P, Z], F32)
         rel_offset = ring("rel_offset", TILES, [P, Z], F32)
         row_sum = ring("row_sum", TILES, [P, Z], F32)
-        log_row_sum = ring("log_row_sum", TILES, [P, Z], F32)
-        neg_log_row_sum = ring("neg_log_row_sum", TILES, [P, Z], F32)
-
+        log_row_sum = ring("log_row_sum", LAST, [P, Z], F32)
+        neg_log_row_sum = ring("neg_log_row_sum", LAST, [P, Z], F32)
         last_norm = one("last_norm", [P, Z], F32)
         last_weight = one("last_weight", [P, Z], F32)
 
-        def exists(i):
-            return 0 <= i < TILES
-
         def neg_logits_of(i, z):
             return neg_logits[z if z > 0 else Z * (i % 2)]
+
+        def term_of(i, z):
+            return terms[(i % 2) * Z + z]
 
         def half(h):
             return slice(h * BANK, (h + 1) * BANK)
@@ -132,23 +138,25 @@ def tile_ragtokendocumentmarginal_t_kernel(tc, x_bytes, x_scale, w1, b1, g, e, s
                 in_=w_raw[:].rearrange("p j (m t) -> p t m j", t=PACK),
             )
 
-        def group_e(copy, h):
-            copy(out=e_grouped[h][:].rearrange("p (n j) -> p n j", j=PACK), in_=e_raw[h][:].rearrange("p j n -> p n j"))
+        def group_e(h):
+            nc.vector.tensor_copy(
+                out=e_grouped[h][:].rearrange("p (n j) -> p n j", j=PACK), in_=e_raw[h][:].rearrange("p j n -> p n j")
+            )
 
         def quantize(codes, scales, grouped):
             nc.vector.quantize_mx(out=codes[:].bitcast(FP8X4), scales=scales[:], in_=grouped[:])
 
-        def prior_shift():
+        def shift_scores():
             nc.vector.tensor_reduce(out=score_max[:], in_=score_sb[:], axis=AX.X, op=ALU.max)
             nc.vector.tensor_tensor(
                 out=score_shifted[:], in0=score_sb[:], in1=score_max[:].unsqueeze(2).to_broadcast([P, TILES, Z]), op=ALU.subtract
             )
             nc.scalar.activation(out=score_exp[:], in_=score_shifted[:], func=ACT.Exp)
 
-        def prior_sum():
+        def sum_scores():
             nc.vector.tensor_reduce(out=score_sum[:], in_=score_exp[:], axis=AX.X, op=ALU.add)
 
-        def prior_finish():
+        def norm_scores():
             nc.vector.tensor_scalar(out=score_norm[:], in0=score_sum[:], scalar1=1.0 / V, scalar2=None, op0=ALU.mult)
 
         def scale_x(i):
@@ -159,30 +167,38 @@ def tile_ragtokendocumentmarginal_t_kernel(tc, x_bytes, x_scale, w1, b1, g, e, s
                 op=ALU.mult,
             )
 
-        def front_bank(i, b):
-            return act_banks[b if i == 1 else 2 + b]
+        def hidden_bank(i, b):
+            return act_banks[b if i == 1 else HALVES + b]
 
         def turn_x(i, b):
             words = x_rows[i % 2][:].bitcast(F32)
             for z in range(2 * b, 2 * b + 2):
                 for u in range(2):
                     nc.tensor.transpose(
-                        front_bank(i, b)[:, block(2 * (z % 2) + u)],
+                        hidden_bank(i, b)[:, block(2 * (z % 2) + u)],
                         words[:, z * D // 2 + u : (z + 1) * D // 2 : 2],
                         identity[:],
                     )
 
         def group_x(i):
             words = x_grouped[i % 2][:].bitcast(F32)
-            for b in range(2):
+            for b in range(PAIRS):
                 nc.scalar.copy(
                     out=words[:, half(b)].rearrange("p (z r u) -> p z r u", z=2, u=2),
-                    in_=front_bank(i, b)[:].rearrange("p (z u r) -> p z r u", z=2, u=2),
+                    in_=hidden_bank(i, b)[:].rearrange("p (z u r) -> p z r u", z=2, u=2),
                 )
+
+        def turn_and_group_x(i):
+            for b in range(PAIRS):
+                turn_x(i, b)
+            group_x(i)
+
+        def quantize_x(i):
+            quantize(x_codes[i % 2], x_scales[i % 2], x_grouped[i % 2])
 
         def first_product(i, t):
             nc.tensor.matmul_mx(
-                out=front_bank(i, t % 2)[:],
+                out=hidden_bank(i, t % 2)[:],
                 lhsT=w_codes[:, block(t)].bitcast(FP8X4),
                 lhsT_scale=w_scales[:, block(t)],
                 rhs=x_codes[i % 2][:].bitcast(FP8X4),
@@ -192,201 +208,7 @@ def tile_ragtokendocumentmarginal_t_kernel(tc, x_bytes, x_scale, w1, b1, g, e, s
             )
 
         def activate(i, t):
-            nc.scalar.activation(out=hidden[i % 2][:, t, :], in_=front_bank(i, t % 2)[:], func=ACT.Tanh, bias=bias_cols[:, t : t + 1])
-
-        def apply_gain(engine, i):
-            engine.tensor_tensor(
-                out=a_grouped[:].rearrange("p (r t) -> p r t", t=PACK),
-                in0=hidden[i % 2][:].rearrange("p t r -> p r t"),
-                in1=gain_cols[:].unsqueeze(1).to_broadcast([P, ROWS, PACK]),
-                op=ALU.mult,
-            )
-
-        def logits(bank, i, z, h):
-            nc.tensor.matmul_mx(
-                out=bank[:],
-                lhsT=a_codes[i % 4][:, block(z)].bitcast(FP8X4),
-                lhsT_scale=a_scales[i % 4][:, block(z)],
-                rhs=e_codes[h][:].bitcast(FP8X4),
-                rhs_scale=e_scales[h][:],
-                start=True,
-                stop=True,
-            )
-
-        def take_max(bank, i, z, h):
-            nc.vector.tensor_scalar(
-                out=neg_logits_of(i, z)[:, half(h)],
-                in0=bank[:],
-                scalar1=-1.0,
-                scalar2=None,
-                op0=ALU.mult,
-                op1=ALU.min,
-                accum_out=neg_half_max[i][:, z, h : h + 1],
-            )
-
-        def shift_logits(bank, i, z, h):
-            nc.vector.scalar_tensor_tensor(
-                out=terms[(i % 2) * Z + z][:, half(h)],
-                in0=bank[:],
-                scalar=rel_offset[i][:, z : z + 1],
-                in1=neg_shift[i % 4][:, half(h)],
-                op0=ALU.add,
-                op1=ALU.add,
-            )
-
-        def turn_back(bank, i, z, h):
-            for j in range(BLOCKS):
-                nc.tensor.transpose(bank[:, block(j)], log_sum_t[i % 2][:, block(h * BLOCKS + j)], identity[:])
-
-        def finish(bank, i, z, h):
-            nc.vector.scalar_tensor_tensor(
-                out=result[i % 2][:, half(h)],
-                in0=bank[:],
-                scalar=offset[i][:, 0:1],
-                in1=neg_shift[i % 4][:, half(h)],
-                op0=ALU.add,
-                op1=ALU.subtract,
-            )
-            nc.sync.dma_start(out=out_tiles[i][:, half(h)], in_=result[i % 2][:, half(h)])
-
-        last = TILES - 1
-        steps = range(TILES + 2)
-
-        def next_log_step(s):
-            return min(x for x in LOG_STEPS if x >= s)
-
-        def spread(ready):
-            when = []
-            for i in range(TILES):
-                when.append(max(ready[i], min(when[-1] + 1, TILES - 2)) if when else ready[i])
-            return when
-
-        mix_step = spread([next_log_step(i) + 1 for i in range(last)] + [TILES])
-        finish_step = spread([next_log_step(mix_step[i]) + 1 for i in range(TILES)])
-
-        def mixed_in(s):
-            return [i for i in range(TILES) if mix_step[i] == s]
-
-        def finished_in(s):
-            return [i for i in range(TILES) if finish_step[i] == s]
-
-        def sum_bank(i, h):
-            return act_banks[HALVES * (1 if i == last else mixed_in(mix_step[i]).index(i)) + h]
-
-        def step_jobs(s):
-            jobs = [(logits, shift_logits, i, z, h) for i in mixed_in(s) for z in range(1, Z) for h in range(HALVES)]
-            if exists(s):
-                jobs.extend((logits, take_max, s, z, h) for z in range(Z) for h in range(HALVES))
-            jobs.extend((turn_back, finish, i, 0, h) for i in finished_in(s) for h in range(HALVES))
-            return jobs
-
-        all_jobs = [(s, job) for s in steps for job in step_jobs(s)]
-        count = {"filled": 0, "emptied": 0, "quantized": -1}
-
-        def fill_ahead(s):
-            while count["filled"] < min(count["emptied"] + RING, len(all_jobs)):
-                job_step, (fill, empty, i, z, h) = all_jobs[count["filled"]]
-                if job_step > s and (empty == finish or i > count["quantized"]):
-                    break
-                fill(vec_banks[count["filled"] % RING], i, z, h)
-                count["filled"] = count["filled"] + 1
-
-        def empty_jobs(s, number):
-            for k in range(number):
-                fill_ahead(s)
-                job_step, (fill, empty, i, z, h) = all_jobs[count["emptied"]]
-                empty(vec_banks[count["emptied"] % RING], i, z, h)
-                count["emptied"] = count["emptied"] + 1
-            fill_ahead(s)
-
-        def row_max(i):
-            nc.vector.tensor_reduce(out=neg_max[i][:], in_=neg_half_max[i][:], axis=AX.X, op=ALU.min)
-
-        def row_offset(i):
-            nc.vector.tensor_tensor(out=offset[i][:], in0=neg_max[i][:], in1=score_shifted[:, i, :], op=ALU.add)
-
-        def row_rel_offset(i):
-            nc.vector.tensor_scalar(
-                out=rel_offset[i][:], in0=offset[i][:], scalar1=offset[i][:, 0:1], scalar2=None, op0=ALU.subtract
-            )
-
-        def fold_shift(i, z, h):
-            so_far = neg_logits_of(i, 0) if z == 1 else neg_shift[i % 4]
-            nc.vector.scalar_tensor_tensor(
-                out=neg_shift[i % 4][:, half(h)],
-                in0=neg_logits_of(i, z)[:, half(h)],
-                scalar=rel_offset[i][:, z : z + 1],
-                in1=so_far[:, half(h)],
-                op0=ALU.subtract,
-                op1=ALU.min,
-            )
-
-        def sum_row(i, z):
-            nc.scalar.activation(
-                out=exp_unused[z % 2][:],
-                in_=neg_logits_of(i, z)[:],
-                func=ACT.Exp,
-                scale=-1.0,
-                bias=neg_max[i][:, z : z + 1],
-                accum_out=row_sum[i][:, z : z + 1],
-            )
-
-        def shift_first_document(i):
-            nc.gpsimd.tensor_tensor(out=terms[(i % 2) * Z][:], in0=neg_shift[i % 4][:], in1=neg_logits_of(i, 0)[:], op=ALU.subtract)
-
-        def exp_term(i, z):
-            tile = terms[(i % 2) * Z + z]
-            if i < last:
-                nc.scalar.activation(out=tile[:], in_=tile[:], func=ACT.Exp, bias=neg_log_row_sum[i][:, z : z + 1])
-            else:
-                nc.scalar.activation(out=tile[:], in_=tile[:], func=ACT.Exp)
-
-        def last_weights():
-            nc.vector.tensor_scalar(
-                out=last_norm[:], in0=row_sum[last][:], scalar1=score_norm[:, last : last + 1], scalar2=None, op0=ALU.mult
-            )
-            nc.vector.reciprocal(out=last_weight[:], in_=last_norm[:])
-
-        def weigh_last_term(z):
-            tile = terms[(last % 2) * Z + z]
-            nc.vector.tensor_scalar(out=tile[:], in0=tile[:], scalar1=last_weight[:, z : z + 1], scalar2=None, op0=ALU.mult)
-
-        def add_term(i, z):
-            for h in range(HALVES):
-                for j in range(BLOCKS):
-                    nc.tensor.matmul(
-                        out=sum_bank(i, h)[:, block(j)],
-                        lhsT=terms[(i % 2) * Z + z][:, block(h * BLOCKS + j)],
-                        rhs=identity[:],
-                        is_transpose=True,
-                        start=(z == TERM_ORDER[0] and j == 0),
-                        stop=(z == TERM_ORDER[-1] and j == BLOCKS - 1),
-                    )
-
-        def logarithms(s):
-            rows = [i for i in range(last) if next_log_step(i) == s]
-            for i in rows:
-                nc.scalar.activation(out=log_row_sum[i][:], in_=row_sum[i][:], func=ACT.Ln, scale=score_norm[:, i : i + 1])
-            for i in range(TILES):
-                if mix_step[i] < min(s, last) and s == next_log_step(mix_step[i]):
-                    nc.scalar.activation(out=log_sum_t[i % 2][:], in_=log_sum_t[i % 2][:], func=ACT.Ln)
-            for i in mixed_in(s) if s < TILES else mixed_in(last) + mixed_in(s):
-                for h in range(HALVES):
-                    nc.scalar.activation(out=log_sum_t[i % 2][:, half(h)], in_=sum_bank(i, h)[:], func=ACT.Ln)
-            for i in rows:
-                nc.scalar.activation(out=neg_log_row_sum[i][:], in_=log_row_sum[i][:], func=ACT.Copy, scale=-1.0)
-
-        def park_sums(s):
-            for i in mixed_in(s):
-                for h in range(HALVES):
-                    nc.scalar.copy(out=log_sum_t[i % 2][:, half(h)], in_=sum_bank(i, h)[:])
-
-        def quantize_x(i):
-            quantize(x_codes[i % 2], x_scales[i % 2], x_grouped[i % 2])
-
-        def quantize_a(i):
-            quantize(a_codes[i % 4], a_scales[i % 4], a_grouped)
-            count["quantized"] = i
+            nc.scalar.activation(out=hidden[i % 2][:, t, :], in_=hidden_bank(i, t % 2)[:], func=ACT.Tanh, bias=bias_cols[:, t : t + 1])
 
         def hidden_first_half(i):
             for t in range(2):
@@ -399,101 +221,300 @@ def tile_ragtokendocumentmarginal_t_kernel(tc, x_bytes, x_scale, w1, b1, g, e, s
             for t in range(2, PACK):
                 activate(i, t)
 
+        def apply_gain(engine, i):
+            engine.tensor_tensor(
+                out=a_grouped[:].rearrange("p (r t) -> p r t", t=PACK),
+                in0=hidden[i % 2][:].rearrange("p t r -> p r t"),
+                in1=gain_cols[:].unsqueeze(1).to_broadcast([P, ROWS, PACK]),
+                op=ALU.mult,
+            )
+
+        log_steps = list(range(1, CATCH_UP, 2)) + [CATCH_UP]
+
+        def mixed_in(s):
+            if s == LAST:
+                return [s - 1]
+            if s == CATCH_UP:
+                return [s - MIX_LAG, s - 1]
+            return [s - MIX_LAG] if s >= MIX_LAG else []
+
+        def finished_in(s):
+            if s >= CATCH_UP:
+                first = CATCH_UP - FINISH_LAG + 2 * (s - CATCH_UP)
+                return [first, first + 1]
+            return [s - FINISH_LAG] if s >= FINISH_LAG else []
+
+        def sum_bank(i, h):
+            return act_banks[(HALVES if i == CATCH_UP - 1 else 0) + h]
+
+        def logits(bank, i, z, h):
+            nc.tensor.matmul_mx(
+                out=bank,
+                lhsT=a_codes[i % LIVE][:, block(z)].bitcast(FP8X4),
+                lhsT_scale=a_scales[i % LIVE][:, block(z)],
+                rhs=e_codes[h][:].bitcast(FP8X4),
+                rhs_scale=e_scales[h][:],
+                start=True,
+                stop=True,
+            )
+
+        def take_max(bank, i, z, h):
+            nc.vector.tensor_scalar(
+                out=neg_logits_of(i, z)[:, half(h)],
+                in0=bank,
+                scalar1=-1.0,
+                scalar2=None,
+                op0=ALU.mult,
+                op1=ALU.min,
+                accum_out=neg_half_max[i][:, z, h : h + 1],
+            )
+
+        def shift_logits(bank, i, z, h):
+            nc.vector.scalar_tensor_tensor(
+                out=term_of(i, z)[:, half(h)],
+                in0=bank,
+                scalar=rel_offset[i][:, z : z + 1],
+                in1=neg_shift[i % LIVE][:, half(h)],
+                op0=ALU.add,
+                op1=ALU.add,
+            )
+
+        def turn_back(bank, i, z, h):
+            for j in range(BLOCKS):
+                nc.tensor.transpose(bank[:, block(j)], log_sum[i % 2][:, block(h * BLOCKS + j)], identity[:])
+
+        def finish(logs, i, z, h):
+            nc.vector.scalar_tensor_tensor(
+                out=result[i % 2][:, half(h)],
+                in0=logs,
+                scalar=offset[i][:, z : z + 1],
+                in1=neg_shift[i % LIVE][:, half(h)],
+                op0=ALU.add,
+                op1=ALU.subtract,
+            )
+            nc.sync.dma_start(out=out_tiles[i][:, half(h)], in_=result[i % 2][:, half(h)])
+
+        def shift_jobs(s, tiles):
+            return [(s, logits, shift_logits, i, z, h) for i in tiles for z in range(1, Z) for h in range(HALVES)]
+
+        def finish_jobs(s, tiles):
+            return [(s, turn_back, finish, i, 0, h) for i in tiles for h in range(HALVES)]
+
+        jobs = []
+        for s in range(TILES):
+            jobs.extend(shift_jobs(s, mixed_in(s)))
+            jobs.extend((s, logits, take_max, s, z, h) for z in range(Z) for h in range(HALVES))
+            jobs.extend(finish_jobs(s, finished_in(s)))
+        jobs.extend(shift_jobs(TILES, [LAST]))
+        jobs.extend(finish_jobs(TILES + 1, [LAST - 1]))
+        progress = {"filled": 0, "emptied": 0, "quantized": -1}
+
+        def fill_ahead(s):
+            while progress["filled"] < min(progress["emptied"] + RING, len(jobs)):
+                job_step, fill, empty, i, z, h = jobs[progress["filled"]]
+                if job_step > s and (fill == turn_back or i > progress["quantized"]):
+                    break
+                fill(vec_banks[progress["filled"] % RING][:], i, z, h)
+                progress["filled"] = progress["filled"] + 1
+
+        def empty_banks(s, number):
+            for k in range(number):
+                fill_ahead(s)
+                job_step, fill, empty, i, z, h = jobs[progress["emptied"]]
+                empty(vec_banks[progress["emptied"] % RING][:], i, z, h)
+                progress["emptied"] = progress["emptied"] + 1
+            fill_ahead(s)
+
+        def quantize_a(i):
+            quantize(a_codes[i % LIVE], a_scales[i % LIVE], a_grouped)
+            progress["quantized"] = i
+
+        def row_max(i):
+            nc.vector.tensor_reduce(out=neg_max[i][:], in_=neg_half_max[i][:], axis=AX.X, op=ALU.min)
+
+        def row_offset(i):
+            nc.vector.tensor_tensor(out=offset[i][:], in0=neg_max[i][:], in1=score_shifted[:, i, :], op=ALU.add)
+
+        def row_rel_offset(i):
+            nc.vector.tensor_scalar(
+                out=rel_offset[i][:], in0=offset[i][:], scalar1=offset[i][:, 0:1], scalar2=None, op0=ALU.subtract
+            )
+
+        def sum_row(i, z):
+            nc.scalar.activation(
+                out=exp_unused[z % 2][:],
+                in_=neg_logits_of(i, z)[:],
+                func=ACT.Exp,
+                scale=-1.0,
+                bias=neg_max[i][:, z : z + 1],
+                accum_out=row_sum[i][:, z : z + 1],
+            )
+
+        def make_shift(i):
+            for z in range(1, Z):
+                so_far = neg_logits_of(i, 0) if z == 1 else neg_shift[i % LIVE]
+                for h in range(HALVES):
+                    nc.vector.scalar_tensor_tensor(
+                        out=neg_shift[i % LIVE][:, half(h)],
+                        in0=neg_logits_of(i, z)[:, half(h)],
+                        scalar=rel_offset[i][:, z : z + 1],
+                        in1=so_far[:, half(h)],
+                        op0=ALU.subtract,
+                        op1=ALU.min,
+                    )
+
+        def shift_first_document(engine, i):
+            engine.tensor_tensor(out=term_of(i, 0)[:], in0=neg_shift[i % LIVE][:], in1=neg_logits_of(i, 0)[:], op=ALU.subtract)
+
+        def exp_terms(i):
+            for z in TERM_ORDER:
+                nc.scalar.activation(out=term_of(i, z)[:], in_=term_of(i, z)[:], func=ACT.Exp, bias=neg_log_row_sum[i][:, z : z + 1])
+
+        def add_terms(i, documents):
+            for z in documents:
+                for h in range(HALVES):
+                    for j in range(BLOCKS):
+                        nc.tensor.matmul(
+                            out=sum_bank(i, h)[:, block(j)],
+                            lhsT=term_of(i, z)[:, block(h * BLOCKS + j)],
+                            rhs=identity[:],
+                            is_transpose=True,
+                            start=(z == TERM_ORDER[0] and j == 0),
+                            stop=(z == TERM_ORDER[-1] and j == BLOCKS - 1),
+                        )
+
+        def log_of_banks(i):
+            for h in range(HALVES):
+                nc.scalar.activation(out=log_sum[i % 2][:, half(h)], in_=sum_bank(i, h)[:], func=ACT.Ln)
+
+        def logarithms(s):
+            since_last = [s] if s - 1 in log_steps else [s - 1, s]
+            for i in since_last:
+                nc.scalar.activation(out=log_row_sum[i][:], in_=row_sum[i][:], func=ACT.Ln, scale=score_norm[:, i : i + 1])
+            for parked_in in since_last[:-1]:
+                for i in mixed_in(parked_in):
+                    nc.scalar.activation(out=log_sum[i % 2][:], in_=log_sum[i % 2][:], func=ACT.Ln)
+            for i in mixed_in(s):
+                log_of_banks(i)
+            for i in since_last:
+                nc.scalar.activation(out=neg_log_row_sum[i][:], in_=log_row_sum[i][:], func=ACT.Copy, scale=-1.0)
+
+        def park_sums(s):
+            for i in mixed_in(s):
+                for h in range(HALVES):
+                    nc.scalar.copy(out=log_sum[i % 2][:, half(h)], in_=sum_bank(i, h)[:])
+
         spread_x_scale()
-        prior_shift()
+        shift_scores()
         scale_x(0)
-        for b in range(2):
-            turn_x(0, b)
-        group_x(0)
-        prior_sum()
+        turn_and_group_x(0)
+        sum_scores()
         group_w()
-        prior_finish()
+        norm_scores()
         quantize(w_codes, w_scales, w_grouped)
         scale_x(1)
-        for b in range(2):
+        for b in range(PAIRS):
             turn_x(1, b)
         quantize_x(0)
         group_x(1)
         hidden_first_half(0)
         hidden_second_half(0)
-        group_e(nc.vector.tensor_copy, 0)
+        for h in range(HALVES):
+            group_e(h)
         quantize_x(1)
-        group_e(nc.vector.tensor_copy, 1)
+        for h in range(HALVES):
+            quantize(e_codes[h], e_scales[h], e_grouped[h])
         hidden_first_half(1)
         hidden_second_half(1)
         apply_gain(nc.vector, 0)
-        for h in range(HALVES):
-            quantize(e_codes[h], e_scales[h], e_grouped[h])
         quantize_a(0)
 
-        for s in steps:
-            if exists(s - 1):
-                shift_first_document(s - 1)
-            if exists(s + 1):
+        for s in range(TILES):
+            mixed, finished = mixed_in(s), finished_in(s)
+            ahead = s + 2
+            if s > 0:
+                shift_first_document(nc.gpsimd if mixed else nc.vector, s - 1)
+            if s < LAST:
                 apply_gain(nc.gpsimd, s + 1)
-            for b in range(2):
-                if mixed_in(s):
-                    empty_jobs(s, HALVES)
-                if s > 0 and exists(s + 2):
-                    turn_x(s + 2, b)
-            if s > 0 and exists(s + 2):
-                group_x(s + 2)
-            if mixed_in(s):
-                empty_jobs(s, (Z - 1) * HALVES * len(mixed_in(s)) - 2 * HALVES)
-            for i in mixed_in(s):
-                for z in TERM_ORDER:
-                    exp_term(i, z)
-            if exists(s):
-                empty_jobs(s, 4)
-                for z in TERM_ORDER[:2]:
-                    empty_jobs(s, 2)
-                    for i in mixed_in(s)[:1]:
-                        add_term(i, z)
-            if finished_in(s):
-                empty_jobs(s, 1)
-            if exists(s):
-                row_max(s)
-            if finished_in(s):
-                empty_jobs(s, HALVES - 1)
-            if s == TILES:
-                last_weights()
-            for i in mixed_in(s):
-                for z in TERM_ORDER[2 if exists(s) and i == mixed_in(s)[0] else 0 :]:
-                    if i == last:
-                        weigh_last_term(z)
-                    add_term(i, z)
-            if exists(s):
-                row_offset(s)
-                for z in range(Z - 1):
-                    sum_row(s, z)
+
+            for b in range(PAIRS):
+                if mixed:
+                    empty_banks(s, HALVES)
+                if 0 < s < CATCH_UP:
+                    turn_x(ahead, b)
+            if 0 < s < CATCH_UP:
+                group_x(ahead)
+            if mixed:
+                empty_banks(s, ((Z - 1) * len(mixed) - PAIRS) * HALVES)
+            for i in mixed:
+                exp_terms(i)
+            empty_banks(s, (Z - len(EARLY_TERMS)) * HALVES)
+            for z in EARLY_TERMS:
+                empty_banks(s, HALVES)
+                for i in mixed[:1]:
+                    add_terms(i, [z])
+            if finished:
+                empty_banks(s, 1)
+            row_max(s)
+            if finished:
+                empty_banks(s, HALVES - 1)
+            if s == CATCH_UP:
+                add_terms(mixed[0], LATE_TERMS)
+                add_terms(mixed[1], EARLY_TERMS)
+            elif s < LAST:
+                for i in mixed:
+                    add_terms(i, LATE_TERMS)
+
+            row_offset(s)
+            for z in range(Z - 1):
+                sum_row(s, z)
             if s == 0:
-                scale_x(2)
-                for b in range(2):
-                    turn_x(2, b)
-                group_x(2)
-            if s > 0 and exists(s + 2):
-                quantize_x(s + 2)
-                hidden_first_half(s + 2)
-            if exists(s):
-                row_rel_offset(s)
-            if exists(s + 3):
-                scale_x(s + 3)
+                scale_x(ahead)
+                turn_and_group_x(ahead)
+            elif s < CATCH_UP:
+                quantize_x(ahead)
+                hidden_first_half(ahead)
+            row_rel_offset(s)
+            if ahead < LAST:
+                scale_x(ahead + 1)
             if s == 0:
-                quantize_x(s + 2)
-                hidden_first_half(s + 2)
-            if exists(s):
-                sum_row(s, Z - 1)
-            if exists(s + 2):
-                hidden_second_half(s + 2)
-            if exists(s):
-                for z in range(1, Z):
-                    for h in range(HALVES):
-                        fold_shift(s, z, h)
-            if exists(s + 1):
+                quantize_x(ahead)
+                hidden_first_half(ahead)
+            sum_row(s, Z - 1)
+            if s < CATCH_UP:
+                hidden_second_half(ahead)
+            make_shift(s)
+            if s < LAST:
                 quantize_a(s + 1)
-            empty_jobs(s, HALVES * len(finished_in(s)[1:]))
-            fill_ahead(s)
-            if s in LOG_STEPS:
+            empty_banks(s, HALVES * len(finished[1:]))
+            if s == CATCH_UP:
+                add_terms(mixed[1], LATE_TERMS)
+            if s in log_steps:
                 logarithms(s)
-            elif s < last:
+            elif s < LAST:
                 park_sums(s)
+
+        shift_first_document(nc.gpsimd, LAST)
+        empty_banks(TILES, PAIRS * HALVES)
+        nc.vector.tensor_scalar(out=last_norm[:], in0=row_sum[LAST][:], scalar1=score_norm[:, LAST:], scalar2=None, op0=ALU.mult)
+        nc.vector.reciprocal(out=last_weight[:], in_=last_norm[:])
+        empty_banks(TILES, (Z - 1 - PAIRS) * HALVES)
+        for z in TERM_ORDER:
+            nc.scalar.activation(out=term_of(LAST, z)[:], in_=term_of(LAST, z)[:], func=ACT.Exp)
+        add_terms(LAST - 1, LATE_TERMS)
+        last_sum = log_sum[LAST % 2]
+        for z in TERM_ORDER:
+            for h in range(HALVES):
+                term, weight = term_of(LAST, z)[:, half(h)], last_weight[:, z : z + 1]
+                if z == TERM_ORDER[0]:
+                    nc.vector.tensor_scalar(out=last_sum[:, half(h)], in0=term, scalar1=weight, scalar2=None, op0=ALU.mult)
+                else:
+                    nc.vector.scalar_tensor_tensor(
+                        out=last_sum[:, half(h)], in0=term, scalar=weight, in1=last_sum[:, half(h)], op0=ALU.mult, op1=ALU.add
+                    )
+        log_of_banks(LAST - 1)
+        for h in range(HALVES):
+            nc.scalar.activation(out=last_sum[:, half(h)], in_=last_sum[:, half(h)], func=ACT.Ln)
+        empty_banks(TILES + 1, HALVES)
+        for h in range(HALVES):
+            finish(last_sum[:, half(h)], LAST, 0, h)

from contextlib import ExitStack

import concourse.mybir as mybir
from concourse.masks import make_identity

N, Z, D, H, V = 1536, 4, 512, 512, 1024
FLOPS = 2 * N * Z * (D * H + H * V)

F32 = mybir.dt.float32
BF16 = mybir.dt.bfloat16
U32 = mybir.dt.uint32
U8 = mybir.dt.uint8
FP8 = mybir.dt.float8_e4m3fn
FP8X4 = mybir.dt.float8_e4m3fn_x4
ACT = mybir.ActivationFunctionType
ALU = mybir.AluOpType
AX = mybir.AxisListType

P = 128
PACK = 4
BANK = 512
TILES = N // P
LAST = TILES - 1
ROWS = Z * P
HALVES = V // BANK
BLOCKS = BANK // P
PAIRS = Z // 2
RING = 4
LIVE = 4
TERM_ORDER = (1, 2, 0, 3)
EARLY_TERMS = TERM_ORDER[:2]
LATE_TERMS = TERM_ORDER[2:]
MIX_LAG = 2
FINISH_LAG = 4
CATCH_UP = TILES - 2


def tile_ragtokendocumentmarginal_t_kernel(tc, x_bytes, x_scale, w1, b1, g, e, score, out):
    nc = tc.nc
    x_tiles = x_bytes.rearrange("(p i) z d -> i p (z d)", i=TILES)
    out_tiles = out.rearrange("(p i) v -> i p v", i=TILES)

    with ExitStack() as ctx:
        sb = ctx.enter_context(tc.tile_pool(name="sb", bufs=1))
        ps = ctx.enter_context(tc.psum_pool(name="ps", bufs=1))
        ctx.enter_context(tc.manual_schedule())

        def ring(name, count, shape, dtype):
            return [sb.tile(shape, dtype, name="%s%d" % (name, j), align_bytes=64) for j in range(count)]

        def one(name, shape, dtype):
            return sb.tile(shape, dtype, name=name, align_bytes=64)

        vec_banks = [ps.tile([P, BANK], F32, name="vec_bank%d" % j) for j in range(RING)]
        act_banks = [ps.tile([P, BANK], F32, name="act_bank%d" % j) for j in range(2 * HALVES)]

        x_code_bytes = ring("x_code_bytes", TILES, [P, Z * D], U8)
        x_scale_cols = one("x_scale_cols", [P, PACK], F32)
        x_scale_rows = one("x_scale_rows", [P, D], F32)
        w_raw = one("w_raw", [P, PACK, H], BF16)
        w_grouped = one("w_grouped", [P, PACK * H], BF16)
        w_codes = one("w_codes", [P, H], U32)
        w_scales = one("w_scales", [P, H], U8)
        e_raw = ring("e_raw", HALVES, [P, PACK, BANK], BF16)
        e_grouped = ring("e_grouped", HALVES, [P, PACK * BANK], BF16)
        e_codes = ring("e_codes", HALVES, [P, BANK], U32)
        e_scales = ring("e_scales", HALVES, [P, BANK], U8)
        bias_cols = one("bias_cols", [P, PACK], BF16)
        gain_cols = one("gain_cols", [P, PACK], BF16)
        identity = one("identity", [P, P], F32)

        score_sb = one("score_sb", [P, TILES, Z], BF16)
        score_max = one("score_max", [P, TILES], F32)
        score_shifted = one("score_shifted", [P, TILES, Z], F32)
        score_exp = one("score_exp", [P, TILES, Z], F32)
        score_sum = one("score_sum", [P, TILES], F32)
        score_norm = one("score_norm", [P, TILES], F32)

        x_rows = ring("x_rows", 2, [P, Z * D], BF16)
        x_grouped = ring("x_grouped", 2, [P, PACK * ROWS], BF16)
        x_codes = ring("x_codes", 2, [P, ROWS], U32)
        x_scales = ring("x_scales", 2, [P, ROWS], U8)
        hidden = ring("hidden", 2, [P, PACK, ROWS], F32)
        a_grouped = one("a_grouped", [P, PACK * ROWS], BF16)
        a_codes = ring("a_codes", LIVE, [P, ROWS], U32)
        a_scales = ring("a_scales", LIVE, [P, ROWS], U8)
        neg_logits = ring("neg_logits", Z + 1, [P, V], F32)
        exp_unused = ring("exp_unused", 2, [P, V], BF16)
        terms = ring("terms", 2 * Z, [P, V], F32)
        neg_shift = ring("neg_shift", LIVE, [P, V], F32)
        log_sum = ring("log_sum", 2, [P, V], F32)
        result = ring("result", 2, [P, V], F32)
        neg_half_max = ring("neg_half_max", TILES, [P, Z, HALVES], F32)
        neg_max = ring("neg_max", TILES, [P, Z], F32)
        offset = ring("offset", TILES, [P, Z], F32)
        rel_offset = ring("rel_offset", TILES, [P, Z], F32)
        row_sum = ring("row_sum", TILES, [P, Z], F32)
        log_row_sum = ring("log_row_sum", LAST, [P, Z], F32)
        neg_log_row_sum = ring("neg_log_row_sum", LAST, [P, Z], F32)
        last_norm = one("last_norm", [P, Z], F32)
        last_weight = one("last_weight", [P, Z], F32)

        def neg_logits_of(i, z):
            return neg_logits[z if z > 0 else Z * (i % 2)]

        def term_of(i, z):
            return terms[(i % 2) * Z + z]

        def half(h):
            return slice(h * BANK, (h + 1) * BANK)

        def block(j):
            return slice(j * P, (j + 1) * P)

        nc.sync.dma_start(out=x_scale_cols[:], in_=x_scale.rearrange("a b (p j) -> p (a b j)", j=PACK))
        nc.sync.dma_start(out=score_sb[:], in_=score.rearrange("(p i) z -> p i z", i=TILES))
        nc.sync.dma_start(out=x_code_bytes[0][:], in_=x_tiles[0])
        nc.sync.dma_start(out=w_raw[:], in_=w1.rearrange("(p j) c -> p j c", j=PACK))
        nc.sync.dma_start(out=x_code_bytes[1][:], in_=x_tiles[1])
        nc.sync.dma_start(out=bias_cols[:], in_=b1.rearrange("(p t) -> p t", t=PACK))
        nc.sync.dma_start(out=gain_cols[:], in_=g.rearrange("(p t) -> p t", t=PACK))
        for h in range(HALVES):
            nc.sync.dma_start(out=e_raw[h][:], in_=e[:, half(h)].rearrange("(p j) n -> p j n", j=PACK))
        for i in range(2, TILES):
            nc.sync.dma_start(out=x_code_bytes[i][:], in_=x_tiles[i])
        make_identity(nc, identity[:])

        def spread_x_scale():
            for j in range(PACK):
                nc.tensor.transpose(vec_banks[0][:, block(j)], x_scale_cols[:, j : j + 1].to_broadcast([P, P]), identity[:])
            nc.scalar.copy(
                out=x_scale_rows[:].rearrange("p (n j) -> p n j", j=PACK), in_=vec_banks[0][:].rearrange("p (j n) -> p n j", j=PACK)
            )

        def group_w():
            nc.vector.tensor_copy(
                out=w_grouped[:].rearrange("p (t m j) -> p t m j", t=PACK, j=PACK),
                in_=w_raw[:].rearrange("p j (m t) -> p t m j", t=PACK),
            )

        def group_e(h):
            nc.vector.tensor_copy(
                out=e_grouped[h][:].rearrange("p (n j) -> p n j", j=PACK), in_=e_raw[h][:].rearrange("p j n -> p n j")
            )

        def quantize(codes, scales, grouped):
            nc.vector.quantize_mx(out=codes[:].bitcast(FP8X4), scales=scales[:], in_=grouped[:])

        def shift_scores():
            nc.vector.tensor_reduce(out=score_max[:], in_=score_sb[:], axis=AX.X, op=ALU.max)
            nc.vector.tensor_tensor(
                out=score_shifted[:], in0=score_sb[:], in1=score_max[:].unsqueeze(2).to_broadcast([P, TILES, Z]), op=ALU.subtract
            )
            nc.scalar.activation(out=score_exp[:], in_=score_shifted[:], func=ACT.Exp)

        def sum_scores():
            nc.vector.tensor_reduce(out=score_sum[:], in_=score_exp[:], axis=AX.X, op=ALU.add)

        def norm_scores():
            nc.vector.tensor_scalar(out=score_norm[:], in0=score_sum[:], scalar1=1.0 / V, scalar2=None, op0=ALU.mult)

        def scale_x(i):
            nc.vector.tensor_tensor(
                out=x_rows[i % 2][:].rearrange("p (z d) -> p z d", z=Z),
                in0=x_code_bytes[i][:].bitcast(FP8).rearrange("p (z d) -> p z d", z=Z),
                in1=x_scale_rows[:].unsqueeze(1).to_broadcast([P, Z, D]),
                op=ALU.mult,
            )

        def hidden_bank(i, b):
            return act_banks[b if i == 1 else HALVES + b]

        def turn_x(i, b):
            words = x_rows[i % 2][:].bitcast(F32)
            for z in range(2 * b, 2 * b + 2):
                for u in range(2):
                    nc.tensor.transpose(
                        hidden_bank(i, b)[:, block(2 * (z % 2) + u)],
                        words[:, z * D // 2 + u : (z + 1) * D // 2 : 2],
                        identity[:],
                    )

        def group_x(i):
            words = x_grouped[i % 2][:].bitcast(F32)
            for b in range(PAIRS):
                nc.scalar.copy(
                    out=words[:, half(b)].rearrange("p (z r u) -> p z r u", z=2, u=2),
                    in_=hidden_bank(i, b)[:].rearrange("p (z u r) -> p z r u", z=2, u=2),
                )

        def turn_and_group_x(i):
            for b in range(PAIRS):
                turn_x(i, b)
            group_x(i)

        def quantize_x(i):
            quantize(x_codes[i % 2], x_scales[i % 2], x_grouped[i % 2])

        def first_product(i, t):
            nc.tensor.matmul_mx(
                out=hidden_bank(i, t % 2)[:],
                lhsT=w_codes[:, block(t)].bitcast(FP8X4),
                lhsT_scale=w_scales[:, block(t)],
                rhs=x_codes[i % 2][:].bitcast(FP8X4),
                rhs_scale=x_scales[i % 2][:],
                start=True,
                stop=True,
            )

        def activate(i, t):
            nc.scalar.activation(out=hidden[i % 2][:, t, :], in_=hidden_bank(i, t % 2)[:], func=ACT.Tanh, bias=bias_cols[:, t : t + 1])

        def hidden_first_half(i):
            for t in range(2):
                first_product(i, t)
            for t in range(2):
                activate(i, t)
                first_product(i, t + 2)

        def hidden_second_half(i):
            for t in range(2, PACK):
                activate(i, t)

        def apply_gain(engine, i):
            engine.tensor_tensor(
                out=a_grouped[:].rearrange("p (r t) -> p r t", t=PACK),
                in0=hidden[i % 2][:].rearrange("p t r -> p r t"),
                in1=gain_cols[:].unsqueeze(1).to_broadcast([P, ROWS, PACK]),
                op=ALU.mult,
            )

        log_steps = list(range(1, CATCH_UP, 2)) + [CATCH_UP]

        def mixed_in(s):
            if s == LAST:
                return [s - 1]
            if s == CATCH_UP:
                return [s - MIX_LAG, s - 1]
            return [s - MIX_LAG] if s >= MIX_LAG else []

        def finished_in(s):
            if s >= CATCH_UP:
                first = CATCH_UP - FINISH_LAG + 2 * (s - CATCH_UP)
                return [first, first + 1]
            return [s - FINISH_LAG] if s >= FINISH_LAG else []

        def sum_bank(i, h):
            return act_banks[(HALVES if i == CATCH_UP - 1 else 0) + h]

        def logits(bank, i, z, h):
            nc.tensor.matmul_mx(
                out=bank,
                lhsT=a_codes[i % LIVE][:, block(z)].bitcast(FP8X4),
                lhsT_scale=a_scales[i % LIVE][:, block(z)],
                rhs=e_codes[h][:].bitcast(FP8X4),
                rhs_scale=e_scales[h][:],
                start=True,
                stop=True,
            )

        def take_max(bank, i, z, h):
            nc.vector.tensor_scalar(
                out=neg_logits_of(i, z)[:, half(h)],
                in0=bank,
                scalar1=-1.0,
                scalar2=None,
                op0=ALU.mult,
                op1=ALU.min,
                accum_out=neg_half_max[i][:, z, h : h + 1],
            )

        def shift_logits(bank, i, z, h):
            nc.vector.scalar_tensor_tensor(
                out=term_of(i, z)[:, half(h)],
                in0=bank,
                scalar=rel_offset[i][:, z : z + 1],
                in1=neg_shift[i % LIVE][:, half(h)],
                op0=ALU.add,
                op1=ALU.add,
            )

        def turn_back(bank, i, z, h):
            for j in range(BLOCKS):
                nc.tensor.transpose(bank[:, block(j)], log_sum[i % 2][:, block(h * BLOCKS + j)], identity[:])

        def finish(logs, i, z, h):
            nc.vector.scalar_tensor_tensor(
                out=result[i % 2][:, half(h)],
                in0=logs,
                scalar=offset[i][:, z : z + 1],
                in1=neg_shift[i % LIVE][:, half(h)],
                op0=ALU.add,
                op1=ALU.subtract,
            )
            nc.sync.dma_start(out=out_tiles[i][:, half(h)], in_=result[i % 2][:, half(h)])

        def shift_jobs(s, tiles):
            return [(s, logits, shift_logits, i, z, h) for i in tiles for z in range(1, Z) for h in range(HALVES)]

        def finish_jobs(s, tiles):
            return [(s, turn_back, finish, i, 0, h) for i in tiles for h in range(HALVES)]

        jobs = []
        for s in range(TILES):
            jobs.extend(shift_jobs(s, mixed_in(s)))
            jobs.extend((s, logits, take_max, s, z, h) for z in range(Z) for h in range(HALVES))
            jobs.extend(finish_jobs(s, finished_in(s)))
        jobs.extend(shift_jobs(TILES, [LAST]))
        jobs.extend(finish_jobs(TILES + 1, [LAST - 1]))
        progress = {"filled": 0, "emptied": 0, "quantized": -1}

        def fill_ahead(s):
            while progress["filled"] < min(progress["emptied"] + RING, len(jobs)):
                job_step, fill, empty, i, z, h = jobs[progress["filled"]]
                if job_step > s and (fill == turn_back or i > progress["quantized"]):
                    break
                fill(vec_banks[progress["filled"] % RING][:], i, z, h)
                progress["filled"] = progress["filled"] + 1

        def empty_banks(s, number):
            for k in range(number):
                fill_ahead(s)
                job_step, fill, empty, i, z, h = jobs[progress["emptied"]]
                empty(vec_banks[progress["emptied"] % RING][:], i, z, h)
                progress["emptied"] = progress["emptied"] + 1
            fill_ahead(s)

        def quantize_a(i):
            quantize(a_codes[i % LIVE], a_scales[i % LIVE], a_grouped)
            progress["quantized"] = i

        def row_max(i):
            nc.vector.tensor_reduce(out=neg_max[i][:], in_=neg_half_max[i][:], axis=AX.X, op=ALU.min)

        def row_offset(i):
            nc.vector.tensor_tensor(out=offset[i][:], in0=neg_max[i][:], in1=score_shifted[:, i, :], op=ALU.add)

        def row_rel_offset(i):
            nc.vector.tensor_scalar(
                out=rel_offset[i][:], in0=offset[i][:], scalar1=offset[i][:, 0:1], scalar2=None, op0=ALU.subtract
            )

        def sum_row(i, z):
            nc.scalar.activation(
                out=exp_unused[z % 2][:],
                in_=neg_logits_of(i, z)[:],
                func=ACT.Exp,
                scale=-1.0,
                bias=neg_max[i][:, z : z + 1],
                accum_out=row_sum[i][:, z : z + 1],
            )

        def make_shift(i):
            for z in range(1, Z):
                so_far = neg_logits_of(i, 0) if z == 1 else neg_shift[i % LIVE]
                for h in range(HALVES):
                    nc.vector.scalar_tensor_tensor(
                        out=neg_shift[i % LIVE][:, half(h)],
                        in0=neg_logits_of(i, z)[:, half(h)],
                        scalar=rel_offset[i][:, z : z + 1],
                        in1=so_far[:, half(h)],
                        op0=ALU.subtract,
                        op1=ALU.min,
                    )

        def shift_first_document(engine, i):
            engine.tensor_tensor(out=term_of(i, 0)[:], in0=neg_shift[i % LIVE][:], in1=neg_logits_of(i, 0)[:], op=ALU.subtract)

        def exp_terms(i):
            for z in TERM_ORDER:
                nc.scalar.activation(out=term_of(i, z)[:], in_=term_of(i, z)[:], func=ACT.Exp, bias=neg_log_row_sum[i][:, z : z + 1])

        def add_terms(i, documents):
            for z in documents:
                for h in range(HALVES):
                    for j in range(BLOCKS):
                        nc.tensor.matmul(
                            out=sum_bank(i, h)[:, block(j)],
                            lhsT=term_of(i, z)[:, block(h * BLOCKS + j)],
                            rhs=identity[:],
                            is_transpose=True,
                            start=(z == TERM_ORDER[0] and j == 0),
                            stop=(z == TERM_ORDER[-1] and j == BLOCKS - 1),
                        )

        def log_of_banks(i):
            for h in range(HALVES):
                nc.scalar.activation(out=log_sum[i % 2][:, half(h)], in_=sum_bank(i, h)[:], func=ACT.Ln)

        def logarithms(s):
            since_last = [s] if s - 1 in log_steps else [s - 1, s]
            for i in since_last:
                nc.scalar.activation(out=log_row_sum[i][:], in_=row_sum[i][:], func=ACT.Ln, scale=score_norm[:, i : i + 1])
            for parked_in in since_last[:-1]:
                for i in mixed_in(parked_in):
                    nc.scalar.activation(out=log_sum[i % 2][:], in_=log_sum[i % 2][:], func=ACT.Ln)
            for i in mixed_in(s):
                log_of_banks(i)
            for i in since_last:
                nc.scalar.activation(out=neg_log_row_sum[i][:], in_=log_row_sum[i][:], func=ACT.Copy, scale=-1.0)

        def park_sums(s):
            for i in mixed_in(s):
                for h in range(HALVES):
                    nc.scalar.copy(out=log_sum[i % 2][:, half(h)], in_=sum_bank(i, h)[:])

        spread_x_scale()
        shift_scores()
        scale_x(0)
        turn_and_group_x(0)
        sum_scores()
        group_w()
        norm_scores()
        quantize(w_codes, w_scales, w_grouped)
        scale_x(1)
        for b in range(PAIRS):
            turn_x(1, b)
        quantize_x(0)
        group_x(1)
        hidden_first_half(0)
        hidden_second_half(0)
        for h in range(HALVES):
            group_e(h)
        quantize_x(1)
        for h in range(HALVES):
            quantize(e_codes[h], e_scales[h], e_grouped[h])
        hidden_first_half(1)
        hidden_second_half(1)
        apply_gain(nc.vector, 0)
        quantize_a(0)

        for s in range(TILES):
            mixed, finished = mixed_in(s), finished_in(s)
            ahead = s + 2
            if s > 0:
                shift_first_document(nc.gpsimd if mixed else nc.vector, s - 1)
            if s < LAST:
                apply_gain(nc.gpsimd, s + 1)

            for b in range(PAIRS):
                if mixed:
                    empty_banks(s, HALVES)
                if 0 < s < CATCH_UP:
                    turn_x(ahead, b)
            if 0 < s < CATCH_UP:
                group_x(ahead)
            if mixed:
                empty_banks(s, ((Z - 1) * len(mixed) - PAIRS) * HALVES)
            for i in mixed:
                exp_terms(i)
            empty_banks(s, (Z - len(EARLY_TERMS)) * HALVES)
            for z in EARLY_TERMS:
                empty_banks(s, HALVES)
                for i in mixed[:1]:
                    add_terms(i, [z])
            if finished:
                empty_banks(s, 1)
            row_max(s)
            if finished:
                empty_banks(s, HALVES - 1)
            if s == CATCH_UP:
                add_terms(mixed[0], LATE_TERMS)
                add_terms(mixed[1], EARLY_TERMS)
            elif s < LAST:
                for i in mixed:
                    add_terms(i, LATE_TERMS)

            row_offset(s)
            for z in range(Z - 1):
                sum_row(s, z)
            if s == 0:
                scale_x(ahead)
                turn_and_group_x(ahead)
            elif s < CATCH_UP:
                quantize_x(ahead)
                hidden_first_half(ahead)
            row_rel_offset(s)
            if ahead < LAST:
                scale_x(ahead + 1)
            if s == 0:
                quantize_x(ahead)
                hidden_first_half(ahead)
            sum_row(s, Z - 1)
            if s < CATCH_UP:
                hidden_second_half(ahead)
            make_shift(s)
            if s < LAST:
                quantize_a(s + 1)
            empty_banks(s, HALVES * len(finished[1:]))
            if s == CATCH_UP:
                add_terms(mixed[1], LATE_TERMS)
            if s in log_steps:
                logarithms(s)
            elif s < LAST:
                park_sums(s)

        shift_first_document(nc.gpsimd, LAST)
        empty_banks(TILES, PAIRS * HALVES)
        nc.vector.tensor_scalar(out=last_norm[:], in0=row_sum[LAST][:], scalar1=score_norm[:, LAST:], scalar2=None, op0=ALU.mult)
        nc.vector.reciprocal(out=last_weight[:], in_=last_norm[:])
        empty_banks(TILES, (Z - 1 - PAIRS) * HALVES)
        for z in TERM_ORDER:
            nc.scalar.activation(out=term_of(LAST, z)[:], in_=term_of(LAST, z)[:], func=ACT.Exp)
        add_terms(LAST - 1, LATE_TERMS)
        last_sum = log_sum[LAST % 2]
        for z in TERM_ORDER:
            for h in range(HALVES):
                term, weight = term_of(LAST, z)[:, half(h)], last_weight[:, z : z + 1]
                if z == TERM_ORDER[0]:
                    nc.vector.tensor_scalar(out=last_sum[:, half(h)], in0=term, scalar1=weight, scalar2=None, op0=ALU.mult)
                else:
                    nc.vector.scalar_tensor_tensor(
                        out=last_sum[:, half(h)], in0=term, scalar=weight, in1=last_sum[:, half(h)], op0=ALU.mult, op1=ALU.add
                    )
        log_of_banks(LAST - 1)
        for h in range(HALVES):
            nc.scalar.activation(out=last_sum[:, half(h)], in_=last_sum[:, half(h)], func=ACT.Ln)
        empty_banks(TILES + 1, HALVES)
        for h in range(HALVES):
            finish(last_sum[:, half(h)], LAST, 0, h)
